import numpy as np
import ml_dtypes

BF16 = ml_dtypes.bfloat16


def bf(x):
    return np.asarray(x, np.float32).astype(BF16)


def f32(x):
    return np.asarray(x, np.float32)


def f64(x):
    return np.asarray(x).astype(np.float64)


def striped(idx):
    return np.tile(idx.reshape(-1, 16).T, (8, 1))


S, K, M, N, E, Q, V, D = 512, 128, 128, 256, 4, 64, 256, 2


def setup_inputs():
    return {"base": bf(np.random.standard_normal((M, S))), "x": bf(np.random.standard_normal((K, N))), "w": bf(1.5 * np.random.standard_normal((E, K, M)) / np.sqrt(K)), "b": f32(0.5 * np.random.standard_normal((M, 1))), "offs": striped(np.random.permutation(S)[:N])}


def reference(base, x, w, b, offs):
    idx = offs[:16].T.reshape(-1)
    z = f64(base).copy()
    for e in range(E):
        z[:, idx[e * Q : (e + 1) * Q]] += f64(w)[e].T @ f64(x)[:, e * Q : (e + 1) * Q]
    z = np.maximum(z + f64(b), 0.0)
    return z.reshape(M, V, D).max(axis=2)

@@ -1,0 +1,55 @@
+import concourse.mybir as mybir
+from concourse.masks import make_identity
+
+BF16, F32, U16 = mybir.dt.bfloat16, mybir.dt.float32, mybir.dt.uint16
+ADD, MAX = mybir.AluOpType.add, mybir.AluOpType.max
+
+P = 128
+CELLS = 512
+POINTS = 256
+SENSORS = 4
+PIECE = POINTS // SENSORS
+POOLED = CELLS // 2
+LIST_COLS = POINTS // 16
+PIECE_COLS = PIECE // 16
+
+FLOPS = 2 * P * P * POINTS
+
+
+def tile_rows_unpool_max_relu_kernel(tc, base, x, w, b, offs, out):
+    nc = tc.nc
+    with (
+        tc.tile_pool(name="held", bufs=1) as held,
+        tc.psum_pool(name="psum", bufs=1) as psum,
+    ):
+        base_tile = held.tile([P, CELLS], BF16, name="base_tile")
+        weights = held.tile([P, SENSORS * P], BF16, name="weights")
+        points = held.tile([P, POINTS], BF16, name="points")
+        offsets = held.tile([P, LIST_COLS], U16, name="offsets")
+        bias = held.tile([P, 1], F32, name="bias")
+        identity = held.tile([P, P], BF16, name="identity")
+        odd = held.tile([P, POOLED], F32, name="odd")
+        pooled = held.tile([P, POOLED], F32, name="pooled")
+        window = psum.tile([P, CELLS], F32, name="window")
+
+        nc.sync.dma_start(base_tile[:], base)
+        nc.sync.dma_start(weights[:].rearrange("k (e m) -> k e m", e=SENSORS), w.rearrange("e k m -> k e m"))
+        nc.sync.dma_start(points[:], x)
+        nc.sync.dma_start(offsets[:], offs)
+        nc.sync.dma_start(bias[:], b)
+        make_identity(nc, identity[:])
+
+        nc.tensor.matmul(window[:], identity[:], base_tile[:], start=True, stop=False)
+
+        for e in range(SENSORS):
+            nc.tensor.matmul(
+                window[:].indirect(offsets[:, e * PIECE_COLS : (e + 1) * PIECE_COLS]),
+                weights[:, e * P : (e + 1) * P],
+                points[:, e * PIECE : (e + 1) * PIECE],
+                start=False,
+                stop=e == SENSORS - 1,
+            )
+
+        nc.vector.tensor_scalar(odd[:], window[:, 1::2], bias[:], 0.0, ADD, MAX)
+        nc.vector.scalar_tensor_tensor(pooled[:], window[:, 0::2], bias[:], odd[:], ADD, MAX)
+        nc.sync.dma_start(out, pooled[:])

@@ -13,6 +13,8 @@ POOLED = CELLS // 2
 LIST_COLS = POINTS // 16
 PIECE_COLS = PIECE // 16
 
+WARM_UPS = 4
+
 FLOPS = 2 * P * P * POINTS
 
 
@@ -31,6 +33,8 @@ def tile_rows_unpool_max_relu_kernel(tc, base, x, w, b, offs, out):
         odd = held.tile([P, POOLED], F32, name="odd")
         pooled = held.tile([P, POOLED], F32, name="pooled")
         window = psum.tile([P, CELLS], F32, name="window")
+        zeros = held.tile([P, CELLS], BF16, name="zeros")
+        spare = psum.tile([P, CELLS], F32, name="spare")
 
         nc.sync.dma_start(base_tile[:], base)
         nc.sync.dma_start(weights[:].rearrange("k (e m) -> k e m", e=SENSORS), w.rearrange("e k m -> k e m"))
@@ -38,6 +42,10 @@ def tile_rows_unpool_max_relu_kernel(tc, base, x, w, b, offs, out):
         nc.sync.dma_start(offsets[:], offs)
         nc.sync.dma_start(bias[:], b)
         make_identity(nc, identity[:])
+
+        nc.vector.memset(zeros[:], 0.0)
+        for i in range(WARM_UPS):
+            nc.tensor.matmul(spare[:], zeros[:, :P], zeros[:], start=True, stop=True)
 
         nc.tensor.matmul(window[:], identity[:], base_tile[:], start=True, stop=False)
 

@@ -13,7 +13,7 @@ POOLED = CELLS // 2
 LIST_COLS = POINTS // 16
 PIECE_COLS = PIECE // 16
 
-WARM_UPS = 4
+WARM_UPS = 3
 
 FLOPS = 2 * P * P * POINTS
 
@@ -58,6 +58,10 @@ def tile_rows_unpool_max_relu_kernel(tc, base, x, w, b, offs, out):
                 stop=e == SENSORS - 1,
             )
 
-        nc.vector.tensor_scalar(odd[:], window[:, 1::2], bias[:], 0.0, ADD, MAX)
-        nc.vector.scalar_tensor_tensor(pooled[:], window[:, 0::2], bias[:], odd[:], ADD, MAX)
-        nc.sync.dma_start(out, pooled[:])
+        halves = [slice(h * POOLED // 2, (h + 1) * POOLED // 2) for h in range(2)]
+        pairs = window[:].rearrange("m (v d) -> m v d", d=2)
+        for half in halves:
+            nc.vector.tensor_scalar(odd[:, half], pairs[:, half, 1], bias[:], 0.0, ADD, MAX)
+        for half in halves:
+            nc.vector.scalar_tensor_tensor(pooled[:, half], pairs[:, half, 0], bias[:], odd[:, half], ADD, MAX)
+            nc.sync.dma_start(out[:, half], pooled[:, half])

import concourse.mybir as mybir
from concourse.masks import make_identity

BF16, F32, U16 = mybir.dt.bfloat16, mybir.dt.float32, mybir.dt.uint16
ADD, MAX = mybir.AluOpType.add, mybir.AluOpType.max

P = 128
CELLS = 512
POINTS = 256
SENSORS = 4
PIECE = POINTS // SENSORS
POOLED = CELLS // 2
LIST_COLS = POINTS // 16
PIECE_COLS = PIECE // 16

WARM_UPS = 3

FLOPS = 2 * P * P * POINTS


def tile_rows_unpool_max_relu_kernel(tc, base, x, w, b, offs, out):
    nc = tc.nc
    with (
        tc.tile_pool(name="held", bufs=1) as held,
        tc.psum_pool(name="psum", bufs=1) as psum,
    ):
        base_tile = held.tile([P, CELLS], BF16, name="base_tile")
        weights = held.tile([P, SENSORS * P], BF16, name="weights")
        points = held.tile([P, POINTS], BF16, name="points")
        offsets = held.tile([P, LIST_COLS], U16, name="offsets")
        bias = held.tile([P, 1], F32, name="bias")
        identity = held.tile([P, P], BF16, name="identity")
        odd = held.tile([P, POOLED], F32, name="odd")
        pooled = held.tile([P, POOLED], F32, name="pooled")
        window = psum.tile([P, CELLS], F32, name="window")
        zeros = held.tile([P, CELLS], BF16, name="zeros")
        spare = psum.tile([P, CELLS], F32, name="spare")

        nc.sync.dma_start(base_tile[:], base)
        nc.sync.dma_start(weights[:].rearrange("k (e m) -> k e m", e=SENSORS), w.rearrange("e k m -> k e m"))
        nc.sync.dma_start(points[:], x)
        nc.sync.dma_start(offsets[:], offs)
        nc.sync.dma_start(bias[:], b)
        make_identity(nc, identity[:])

        nc.vector.memset(zeros[:], 0.0)
        for i in range(WARM_UPS):
            nc.tensor.matmul(spare[:], zeros[:, :P], zeros[:], start=True, stop=True)

        nc.tensor.matmul(window[:], identity[:], base_tile[:], start=True, stop=False)

        for e in range(SENSORS):
            nc.tensor.matmul(
                window[:].indirect(offsets[:, e * PIECE_COLS : (e + 1) * PIECE_COLS]),
                weights[:, e * P : (e + 1) * P],
                points[:, e * PIECE : (e + 1) * PIECE],
                start=False,
                stop=e == SENSORS - 1,
            )

        halves = [slice(h * POOLED // 2, (h + 1) * POOLED // 2) for h in range(2)]
        pairs = window[:].rearrange("m (v d) -> m v d", d=2)
        for half in halves:
            nc.vector.tensor_scalar(odd[:, half], pairs[:, half, 1], bias[:], 0.0, ADD, MAX)
        for half in halves:
            nc.vector.scalar_tensor_tensor(pooled[:, half], pairs[:, half, 0], bias[:], odd[:, half], ADD, MAX)
            nc.sync.dma_start(out[:, half], pooled[:, half])
